import numpy as np, ml_dtypes
CORES = [21,29,37,45,53,61,69,77,85]
N = 9
KT, C = 8, 64
def setup_inputs(rng):
    return {"x": rng.standard_normal((N, 128, KT * C), dtype=np.float32).astype(ml_dtypes.bfloat16)}
def setup_inputs_big(rng):
    d = setup_inputs(rng)
    for k in ("x",): d[k] = (d[k].astype(np.float32) * 1024.0).astype(d[k].dtype)
    return d
def setup_inputs_small(rng):
    d = setup_inputs(rng)
    for k in ("x",): d[k] = (d[k].astype(np.float32) * (1 / 1024.0)).astype(d[k].dtype)
    return d
def setup_inputs_apart(rng):
    d = setup_inputs(rng)
    f = (10.0 ** rng.permutation(np.linspace(-1.5, 1.5, N))).astype(np.float32).reshape(N, 1, 1)
    for k in ("x",): d[k] = (d[k].astype(np.float32) * f).astype(d[k].dtype)
    return d
def reference(x):
    X = x.astype(np.float64)
    y = np.full((N, C, N * C), np.nan)
    for r in range(N):
        for i in range(N):
            s = i
            if s != r: y[r][:, C * i:C * i + C] = sum(X[r][:, C * t:C * t + C].T @ X[s][:, C * t:C * t + C] for t in range(KT))
    return {"y": y.astype(ml_dtypes.bfloat16 if x.dtype != np.float64 else np.float64)}

@@ -1,0 +1,205 @@
+from concourse.bass import DstId, RemoteDMATransfer
+
+N, KT, C = 9, 8, 64
+W = KT * C
+
+SAME_PW = True
+CROSS_PW = True
+NQ_AG = 4
+A_ENG = 8
+B_ENG = 8
+F_ENG = 8
+M_ENG = 8
+OTHER_DIE = True
+B_FIRST = False
+SPREAD = False
+NBANK = 8 if not (SAME_PW and CROSS_PW) else 2
+
+SCRATCH = {
+    "X": ("sbuf", [128, N * W], "bfloat16"),
+    "R": ("sbuf", [128, N * C], "bfloat16"),
+}
+for _j in range(NBANK):
+    SCRATCH["ps%d" % _j] = ("psum", [128, 512], "float32")
+
+SEMAPHORES = ["ld", "st", "snd"] + [p + str(a) for p in ("xa", "mm", "cp", "rr") for a in range(N)]
+
+
+def _plan(T, topo):
+    P = list(T.cores)
+    n = len(P)
+    ch = [topo.chip(c) for c in P]
+    every = range(topo.CORES_PER_CHIP * topo.CHIPS)
+    planes = []
+    for r in range(n):
+        for pl in planes:
+            if topo.same_plane(ch[pl[0]], ch[r]):
+                pl.append(r)
+                break
+        else:
+            planes.append([r])
+    role = {}
+
+    def node(c, h):
+        if c not in role:
+            role[c] = {"home": h, "calls": [], "expect": {}, "vis": [], "res": []}
+        return role[c]
+
+    def arrive(c, a, k):
+        role[c]["expect"][a] = role[c]["expect"].get(a, 0) + k
+
+    def host(c, h, v, both, cls):
+        node(c, h)["vis"].append((v, both, cls))
+        if both:
+            role[P[v]]["res"].append((h, 1, cls + 1))
+            if c != P[h]:
+                role[P[h]]["res"].append((v, 0, cls + 1))
+
+    for r in range(n):
+        node(P[r], r)
+
+    def ports(r):
+        far = [P[s] for s in range(n) if s != r and not topo.same_plane(ch[r], ch[s])]
+        own = [c for c in every if topo.chip(c) == ch[r] and c != P[r] and all(topo.may_write(c, o) for o in far)]
+        return sorted(own, key=lambda c: ((topo.die(c) == topo.die(P[r])) == OTHER_DIE, c))
+
+    hosted = {r: [] for r in range(n)}
+    visits = {r: [] for r in range(n)}
+    pa, pb = planes
+    for i, a in enumerate(pa):
+        for j, b in enumerate(pb):
+            if CROSS_PW:
+                h, v = (a, b) if (i + j) % 2 == 0 else (b, a)
+                hosted[h].append(v)
+                visits[v].append(h)
+            else:
+                visits[a].append(b)
+                visits[b].append(a)
+    Q = {}
+    for r in range(n):
+        q = max(len(hosted[r]), len(visits[r])) if CROSS_PW else min(NQ_AG, len(visits[r]))
+        Q[r] = ports(r)[:q]
+        for c in Q[r]:
+            node(c, r)
+            arrive(c, r, A_ENG)
+        role[P[r]]["calls"].append((0, W, list(Q[r]), A_ENG, True))
+    for v in range(n):
+        if CROSS_PW:
+            tgt = [Q[h][hosted[h].index(v)] for h in sorted(visits[v], key=lambda s: topo.mates(ch[v], ch[s]))]
+            q = len(Q[v])
+            pieces = [(0, W, t) for t in tgt]
+            if len(pieces) < q:
+                lo, hi, t = pieces.pop()
+                pieces += [(lo, W // 2, t), (W // 2, hi, t)]
+            for c, (lo, hi, t) in zip(Q[v], pieces):
+                role[c]["calls"].append((lo, hi, [t], F_ENG, False))
+                arrive(t, v, F_ENG)
+        else:
+            order = sorted(visits[v], key=lambda s: (topo.mates(ch[v], ch[s]), (s - v) % n))
+            for k, c in enumerate(Q[v]):
+                mine = order[k::len(Q[v])]
+                role[c]["calls"].append((0, W, [P[s] for s in mine], F_ENG, False))
+                for s in mine:
+                    arrive(P[s], v, F_ENG)
+    for pl in planes:
+        m = len(pl)
+        for i in range(m):
+            to = []
+            for d in range(1, m):
+                if SAME_PW and not (2 * d < m or (2 * d == m and i < d)):
+                    continue
+                to.append(pl[(i + d) % m])
+            role[P[pl[i]]]["calls"].insert(0 if B_FIRST else 1, (0, W, [P[s] for s in to], B_ENG, False))
+            for s in to:
+                arrive(P[s], pl[i], B_ENG)
+                host(P[s], s, pl[i], SAME_PW, 0)
+    for h in range(n):
+        if CROSS_PW:
+            for c, v in zip(Q[h], hosted[h]):
+                host(c, h, v, True, 2)
+        else:
+            for v in sorted(visits[h], key=lambda s: (topo.mates(ch[h], ch[s]), (h - s) % n)):
+                host(P[h], h, v, False, 2)
+    return role
+
+
+def rank_program(g, core, T, topo):
+    role = _plan(T, topo)
+    me = role.get(core)
+    if me is None:
+        return
+    P = list(T.cores)
+    n = len(P)
+    h = me["home"]
+    is_rank = core == P[h]
+    X, R, S = T.X, T.R, T.sem
+    sent = [0]
+    leaves = topo.mask(core, P[(h + 1) % n])
+
+    def xs(a, lo=0, hi=W):
+        return X[:, a * W + lo:a * W + hi]
+
+    def send(src, dsts, sem, neng, high):
+        m = -1
+        for d, _ in dsts:
+            m &= topo.mask(core, d)
+        eng = [b for b in range(m.bit_length()) if (m >> b) & 1]
+        stay = [b for b in eng if not (leaves >> b) & 1]
+        if high and neng <= len(stay):
+            eng = stay
+        if SPREAD and 2 * neng <= len(eng):
+            eng = eng[::2]
+        eng = eng[:neng]
+        ids = [DstId(rid=topo.addr(d)[0], pnc=topo.addr(d)[1]) for d, _ in dsts]
+        tr = RemoteDMATransfer(dst_ids=ids, dma_engine_mask=sum(1 << b for b in eng), remote_sem=sem,
+                               srcs=[src], dsts=[ap for _, ap in dsts], alu_op=0)
+        g.remote_dma_fused([tr], local_sem=S.snd)
+        sent[0] += neng
+
+    if is_rank:
+        g.sync.dma_start(xs(h), T.x[:]).then_inc(S.ld, 16)
+        home = (S.ld, 16)
+    else:
+        home = (S["xa%d" % h], me["expect"][h])
+    g.wait_ge(*home)
+    for lo, hi, dsts, neng, high in me["calls"]:
+        if dsts:
+            send(xs(h, lo, hi), [(d, xs(h, lo, hi)) for d in dsts], S["xa%d" % h], neng, high)
+
+    if me["vis"]:
+        g.tensor.wait_ge(*home)
+    for j, (v, both, _) in enumerate(me["vis"]):
+        ps = T["ps%d" % j]
+        g.tensor.wait_ge(S["xa%d" % v], me["expect"][v])
+        for half in range(2 if both else 1):
+            a, b = (h, v) if half == 0 else (v, h)
+            for t in range(KT):
+                mm = g.tensor.matmul(ps[C * half:C * half + C, 0:C], xs(a, C * t, C * t + C), xs(b, C * t, C * t + C),
+                                     t == 0, t == KT - 1)
+            mm.then_inc(S["mm%d" % v], 1)
+        rows = 2 * C if both else C
+        g.vector.wait_ge(S["mm%d" % v], 2 if both else 1)
+        g.vector.tensor_copy(R[0:rows, C * v:C * v + C], ps[0:rows, 0:C]).then_inc(S["cp%d" % v], 1)
+
+    for v, both, _ in me["vis"]:
+        if both:
+            g.wait_ge(S["cp%d" % v], 1)
+            dsts = [(P[v], R[:, C * h:C * h + C])]
+            if not is_rank:
+                dsts.append((P[h], R[:, C * v:C * v + C]))
+            send(R[:, C * v:C * v + C], dsts, S["rr%d" % ((h + v) % n)], M_ENG, False)
+
+    stores = 0
+    if is_rank:
+        items = [(cls, S["cp%d" % v], 1, 0, v) for v, _, cls in me["vis"]]
+        items += [(cls, S["rr%d" % ((h + p) % n)], M_ENG, half, p) for p, half, cls in me["res"]]
+        items.sort(key=lambda it: (it[0], it[4]))
+        for k, (_, sem, cnt, half, p) in enumerate(items):
+            q = g.sync if k % 2 == 0 else g.scalar
+            q.wait_ge(sem, cnt)
+            q.dma_start(T.y[:, C * p:C * p + C], R[C * half:C * half + C, C * p:C * p + C]).then_inc(S.st, 16)
+            stores += 1
+    if sent[0]:
+        g.wait_ge(S.snd, sent[0])
+    if stores:
+        g.wait_ge(S.st, 16 * stores)

@@ -11,8 +11,10 @@ B_ENG = 8
 F_ENG = 8
 M_ENG = 8
 OTHER_DIE = True
-B_FIRST = False
 SPREAD = False
+CUT = 2 * C
+CH = ((0, CUT), (CUT, W))
+FAM = ("xa", "xb")
 NBANK = 8 if not (SAME_PW and CROSS_PW) else 2
 
 SCRATCH = {
@@ -22,7 +24,7 @@ SCRATCH = {
 for _j in range(NBANK):
     SCRATCH["ps%d" % _j] = ("psum", [128, 512], "float32")
 
-SEMAPHORES = ["ld", "st", "snd"] + [p + str(a) for p in ("xa", "mm", "cp", "rr") for a in range(N)]
+SEMAPHORES = ["ld0", "ld1", "st", "snd"] + [p + str(a) for p in FAM + ("mm", "cp", "rr") for a in range(N)]
 
 
 def _plan(T, topo):
@@ -45,8 +47,8 @@ def _plan(T, topo):
             role[c] = {"home": h, "calls": [], "expect": {}, "vis": [], "res": []}
         return role[c]
 
-    def arrive(c, a, k):
-        role[c]["expect"][a] = role[c]["expect"].get(a, 0) + k
+    def arrive(c, a, k, cnt):
+        role[c]["expect"][(a, k)] = role[c]["expect"].get((a, k), 0) + cnt
 
     def host(c, h, v, both, cls):
         node(c, h)["vis"].append((v, both, cls))
@@ -81,26 +83,26 @@ def _plan(T, topo):
         Q[r] = ports(r)[:q]
         for c in Q[r]:
             node(c, r)
-            arrive(c, r, A_ENG)
-        role[P[r]]["calls"].append((0, W, list(Q[r]), A_ENG, True))
+        for k, (lo, hi) in enumerate(CH):
+            role[P[r]]["calls"].append((k, lo, hi, list(Q[r]), A_ENG, True))
+            for c in Q[r]:
+                arrive(c, r, k, A_ENG)
     for v in range(n):
         if CROSS_PW:
             tgt = [Q[h][hosted[h].index(v)] for h in sorted(visits[v], key=lambda s: topo.mates(ch[v], ch[s]))]
-            q = len(Q[v])
-            pieces = [(0, W, t) for t in tgt]
-            if len(pieces) < q:
-                lo, hi, t = pieces.pop()
-                pieces += [(lo, W // 2, t), (W // 2, hi, t)]
-            for c, (lo, hi, t) in zip(Q[v], pieces):
-                role[c]["calls"].append((lo, hi, [t], F_ENG, False))
-                arrive(t, v, F_ENG)
+            jobs = [([t], [c]) for t, c in zip(tgt, Q[v])]
+            if len(tgt) < len(Q[v]):
+                jobs[-1] = ([tgt[-1]], Q[v][len(tgt) - 1:])
         else:
             order = sorted(visits[v], key=lambda s: (topo.mates(ch[v], ch[s]), (s - v) % n))
-            for k, c in enumerate(Q[v]):
-                mine = order[k::len(Q[v])]
-                role[c]["calls"].append((0, W, [P[s] for s in mine], F_ENG, False))
-                for s in mine:
-                    arrive(P[s], v, F_ENG)
+            jobs = [([P[s] for s in order[k::len(Q[v])]], [c]) for k, c in enumerate(Q[v])]
+        for to, cs in jobs:
+            for k, (lo, hi) in enumerate(CH):
+                step = (hi - lo) // len(cs)
+                for i, c in enumerate(cs):
+                    role[c]["calls"].append((k, lo + i * step, lo + (i + 1) * step, to, F_ENG, False))
+                    for t in to:
+                        arrive(t, v, k, F_ENG)
     for pl in planes:
         m = len(pl)
         for i in range(m):
@@ -109,9 +111,9 @@ def _plan(T, topo):
                 if SAME_PW and not (2 * d < m or (2 * d == m and i < d)):
                     continue
                 to.append(pl[(i + d) % m])
-            role[P[pl[i]]]["calls"].insert(0 if B_FIRST else 1, (0, W, [P[s] for s in to], B_ENG, False))
+            role[P[pl[i]]]["calls"].append((0, 0, W, [P[s] for s in to], B_ENG, False))
             for s in to:
-                arrive(P[s], pl[i], B_ENG)
+                arrive(P[s], pl[i], 0, B_ENG)
                 host(P[s], s, pl[i], SAME_PW, 0)
     for h in range(n):
         if CROSS_PW:
@@ -157,20 +159,28 @@ def rank_program(g, core, T, topo):
         sent[0] += neng
 
     if is_rank:
-        g.sync.dma_start(xs(h), T.x[:]).then_inc(S.ld, 16)
-        home = (S.ld, 16)
+        for k, (lo, hi) in enumerate(CH):
+            (g.sync, g.scalar)[k].dma_start(xs(h, lo, hi), T.x[:, lo:hi]).then_inc(S["ld%d" % k], 16)
+        home = [(S["ld%d" % k], 16) for k in range(len(CH))]
     else:
-        home = (S["xa%d" % h], me["expect"][h])
-    g.wait_ge(*home)
-    for lo, hi, dsts, neng, high in me["calls"]:
+        home = [(S[FAM[k] + str(h)], me["expect"][(h, k)]) for k in range(len(CH))]
+    got = set()
+    for k, lo, hi, dsts, neng, high in me["calls"]:
+        for c, (a, b) in enumerate(CH):
+            if lo < b and hi > a and c not in got:
+                g.wait_ge(*home[c])
+                got.add(c)
         if dsts:
-            send(xs(h, lo, hi), [(d, xs(h, lo, hi)) for d in dsts], S["xa%d" % h], neng, high)
+            send(xs(h, lo, hi), [(d, xs(h, lo, hi)) for d in dsts], S[FAM[k] + str(h)], neng, high)
 
     if me["vis"]:
-        g.tensor.wait_ge(*home)
+        for w in home:
+            g.tensor.wait_ge(*w)
     for j, (v, both, _) in enumerate(me["vis"]):
         ps = T["ps%d" % j]
-        g.tensor.wait_ge(S["xa%d" % v], me["expect"][v])
+        for k in range(len(CH)):
+            if me["expect"].get((v, k)):
+                g.tensor.wait_ge(S[FAM[k] + str(v)], me["expect"][(v, k)])
         for half in range(2 if both else 1):
             a, b = (h, v) if half == 0 else (v, h)
             for t in range(KT):

@@ -3,31 +3,49 @@ from concourse.bass import DstId, RemoteDMATransfer
 N, KT, C = 9, 8, 64
 W = KT * C
 
-SAME_PW = True
-CROSS_PW = True
-NQ_AG = 4
 A_ENG = 8
 B_ENG = 8
 F_ENG = 8
 M_ENG = 8
-OTHER_DIE = True
-SPREAD = False
+NQ = 3
 CUT = 2 * C
 CH = ((0, CUT), (CUT, W))
 FAM = ("xa", "xb")
-NBANK = 8 if not (SAME_PW and CROSS_PW) else 2
 
 SCRATCH = {
     "X": ("sbuf", [128, N * W], "bfloat16"),
     "R": ("sbuf", [128, N * C], "bfloat16"),
+    "MV": ("sbuf", [128, 2 * C], "bfloat16"),
 }
-for _j in range(NBANK):
+for _j in range(4):
     SCRATCH["ps%d" % _j] = ("psum", [128, 512], "float32")
 
-SEMAPHORES = ["ld0", "ld1", "st", "snd"] + [p + str(a) for p in FAM + ("mm", "cp", "rr") for a in range(N)]
+SEMAPHORES = ["ld0", "ld1", "ms", "st", "snd"] + [p + str(a) for p in FAM + ("mv", "mh", "cv", "cw", "rr")
+                                                  for a in range(N)]
+_CACHE = {}
+
+
+def _cross(pa, pb, mate):
+    two = [(x, y) for x in range(len(pb)) for y in range(x + 1, len(pb))]
+    best = None
+    for code in range(len(two) ** len(pa)):
+        rows = []
+        for _ in pa:
+            rows.append(two[code % len(two)])
+            code //= len(two)
+        hin = [sum(1 for j in rows[i] if not mate[i][j]) for i in range(len(pa))]
+        hin += [sum(1 for i in range(len(pa)) if j not in rows[i] and not mate[i][j]) for j in range(len(pb))]
+        out = [sum(1 for j in range(len(pb)) if j not in rows[i] and not mate[i][j]) for i in range(len(pa))]
+        out += [sum(1 for i in range(len(pa)) if j in rows[i] and not mate[i][j]) for j in range(len(pb))]
+        cost = (max(hin), max(out))
+        if best is None or cost < best[0]:
+            best = (cost, rows)
+    return best[1]
 
 
 def _plan(T, topo):
+    if "role" in _CACHE:
+        return _CACHE["role"]
     P = list(T.cores)
     n = len(P)
     ch = [topo.chip(c) for c in P]
@@ -50,12 +68,11 @@ def _plan(T, topo):
     def arrive(c, a, k, cnt):
         role[c]["expect"][(a, k)] = role[c]["expect"].get((a, k), 0) + cnt
 
-    def host(c, h, v, both, cls):
-        node(c, h)["vis"].append((v, both, cls))
-        if both:
-            role[P[v]]["res"].append((h, 1, cls + 1))
-            if c != P[h]:
-                role[P[h]]["res"].append((v, 0, cls + 1))
+    def host(c, h, v):
+        node(c, h)["vis"].append(v)
+        role[P[v]]["res"].append(h)
+        if c != P[h]:
+            role[P[h]]["res"].append(v)
 
     for r in range(n):
         node(P[r], r)
@@ -63,24 +80,20 @@ def _plan(T, topo):
     def ports(r):
         far = [P[s] for s in range(n) if s != r and not topo.same_plane(ch[r], ch[s])]
         own = [c for c in every if topo.chip(c) == ch[r] and c != P[r] and all(topo.may_write(c, o) for o in far)]
-        return sorted(own, key=lambda c: ((topo.die(c) == topo.die(P[r])) == OTHER_DIE, c))
+        return sorted(own, key=lambda c: (topo.die(c) == topo.die(P[r]), c))
 
     hosted = {r: [] for r in range(n)}
     visits = {r: [] for r in range(n)}
     pa, pb = planes
+    rows = _cross(pa, pb, [[topo.mates(ch[a], ch[b]) for b in pb] for a in pa])
     for i, a in enumerate(pa):
         for j, b in enumerate(pb):
-            if CROSS_PW:
-                h, v = (a, b) if (i + j) % 2 == 0 else (b, a)
-                hosted[h].append(v)
-                visits[v].append(h)
-            else:
-                visits[a].append(b)
-                visits[b].append(a)
+            h, v = (a, b) if j in rows[i] else (b, a)
+            hosted[h].append(v)
+            visits[v].append(h)
     Q = {}
     for r in range(n):
-        q = max(len(hosted[r]), len(visits[r])) if CROSS_PW else min(NQ_AG, len(visits[r]))
-        Q[r] = ports(r)[:q]
+        Q[r] = ports(r)[:min(NQ, max(len(hosted[r]), len(visits[r])))]
         for c in Q[r]:
             node(c, r)
         for k, (lo, hi) in enumerate(CH):
@@ -88,40 +101,31 @@ def _plan(T, topo):
             for c in Q[r]:
                 arrive(c, r, k, A_ENG)
     for v in range(n):
-        if CROSS_PW:
-            tgt = [Q[h][hosted[h].index(v)] for h in sorted(visits[v], key=lambda s: topo.mates(ch[v], ch[s]))]
-            jobs = [([t], [c]) for t, c in zip(tgt, Q[v])]
-            if len(tgt) < len(Q[v]):
-                jobs[-1] = ([tgt[-1]], Q[v][len(tgt) - 1:])
-        else:
-            order = sorted(visits[v], key=lambda s: (topo.mates(ch[v], ch[s]), (s - v) % n))
-            jobs = [([P[s] for s in order[k::len(Q[v])]], [c]) for k, c in enumerate(Q[v])]
+        q = len(Q[v])
+        tgt = [Q[h][hosted[h].index(v) % len(Q[h])] for h in sorted(visits[v], key=lambda s: topo.mates(ch[v], ch[s]))]
+        jobs = [(tgt[i::q], [c]) for i, c in enumerate(Q[v])]
+        if len(tgt) < q:
+            jobs = jobs[:len(tgt) - 1] + [([tgt[-1]], Q[v][len(tgt) - 1:])]
         for to, cs in jobs:
             for k, (lo, hi) in enumerate(CH):
-                step = (hi - lo) // len(cs)
-                for i, c in enumerate(cs):
+                cs_k = cs if k == 0 else cs[:1]
+                step = (hi - lo) // len(cs_k)
+                for i, c in enumerate(cs_k):
                     role[c]["calls"].append((k, lo + i * step, lo + (i + 1) * step, to, F_ENG, False))
                     for t in to:
                         arrive(t, v, k, F_ENG)
     for pl in planes:
         m = len(pl)
         for i in range(m):
-            to = []
-            for d in range(1, m):
-                if SAME_PW and not (2 * d < m or (2 * d == m and i < d)):
-                    continue
-                to.append(pl[(i + d) % m])
+            to = [pl[(i + d) % m] for d in range(1, m) if 2 * d < m or (2 * d == m and i < d)]
             role[P[pl[i]]]["calls"].append((0, 0, W, [P[s] for s in to], B_ENG, False))
             for s in to:
                 arrive(P[s], pl[i], 0, B_ENG)
-                host(P[s], s, pl[i], SAME_PW, 0)
+                host(P[s], s, pl[i])
     for h in range(n):
-        if CROSS_PW:
-            for c, v in zip(Q[h], hosted[h]):
-                host(c, h, v, True, 2)
-        else:
-            for v in sorted(visits[h], key=lambda s: (topo.mates(ch[h], ch[s]), (h - s) % n)):
-                host(P[h], h, v, False, 2)
+        for i, v in enumerate(hosted[h]):
+            host(Q[h][i % len(Q[h])], h, v)
+    _CACHE["role"] = role
     return role
 
 
@@ -134,8 +138,9 @@ def rank_program(g, core, T, topo):
     n = len(P)
     h = me["home"]
     is_rank = core == P[h]
-    X, R, S = T.X, T.R, T.sem
+    X, R, MV, S = T.X, T.R, T.MV, T.sem
     sent = [0]
+    lq = (g.sync, g.scalar)
     leaves = topo.mask(core, P[(h + 1) % n])
 
     def xs(a, lo=0, hi=W):
@@ -149,8 +154,6 @@ def rank_program(g, core, T, topo):
         stay = [b for b in eng if not (leaves >> b) & 1]
         if high and neng <= len(stay):
             eng = stay
-        if SPREAD and 2 * neng <= len(eng):
-            eng = eng[::2]
         eng = eng[:neng]
         ids = [DstId(rid=topo.addr(d)[0], pnc=topo.addr(d)[1]) for d, _ in dsts]
         tr = RemoteDMATransfer(dst_ids=ids, dma_engine_mask=sum(1 << b for b in eng), remote_sem=sem,
@@ -158,10 +161,22 @@ def rank_program(g, core, T, topo):
         g.remote_dma_fused([tr], local_sem=S.snd)
         sent[0] += neng
 
+    fills = 0
+    if me["vis"]:
+        g.vector.memset(MV[C:2 * C, :], 0.0).then_inc(S.ms, 1)
+        fills += 1
     if is_rank:
-        for k, (lo, hi) in enumerate(CH):
-            (g.sync, g.scalar)[k].dma_start(xs(h, lo, hi), T.x[:, lo:hi]).then_inc(S["ld%d" % k], 16)
+        g.vector.memset(R[0:C, C * h:C * h + C], 0.0).then_inc(S.ms, 1)
+        fills += 1
+    else:
+        for v in me["vis"]:
+            g.vector.memset(R[C:2 * C, C * v:C * v + C], 0.0).then_inc(S.ms, 1)
+            fills += 1
+
+    if is_rank:
         home = [(S["ld%d" % k], 16) for k in range(len(CH))]
+        for k, (lo, hi) in enumerate(CH):
+            lq[k].dma_start(xs(h, lo, hi), T.x[:, lo:hi]).then_inc(*home[k])
     else:
         home = [(S[FAM[k] + str(h)], me["expect"][(h, k)]) for k in range(len(CH))]
     got = set()
@@ -170,46 +185,43 @@ def rank_program(g, core, T, topo):
             if lo < b and hi > a and c not in got:
                 g.wait_ge(*home[c])
                 got.add(c)
-        if dsts:
-            send(xs(h, lo, hi), [(d, xs(h, lo, hi)) for d in dsts], S[FAM[k] + str(h)], neng, high)
+        send(xs(h, lo, hi), [(d, xs(h, lo, hi)) for d in dsts], S[FAM[k] + str(h)], neng, high)
 
     if me["vis"]:
         for w in home:
             g.tensor.wait_ge(*w)
-    for j, (v, both, _) in enumerate(me["vis"]):
-        ps = T["ps%d" % j]
-        for k in range(len(CH)):
-            if me["expect"].get((v, k)):
-                g.tensor.wait_ge(S[FAM[k] + str(v)], me["expect"][(v, k)])
-        for half in range(2 if both else 1):
-            a, b = (h, v) if half == 0 else (v, h)
-            for t in range(KT):
-                mm = g.tensor.matmul(ps[C * half:C * half + C, 0:C], xs(a, C * t, C * t + C), xs(b, C * t, C * t + C),
-                                     t == 0, t == KT - 1)
-            mm.then_inc(S["mm%d" % v], 1)
-        rows = 2 * C if both else C
-        g.vector.wait_ge(S["mm%d" % v], 2 if both else 1)
-        g.vector.tensor_copy(R[0:rows, C * v:C * v + C], ps[0:rows, 0:C]).then_inc(S["cp%d" % v], 1)
+    for j, v in enumerate(me["vis"]):
+        stages = [(k, range(lo // C, hi // C)) for k, (lo, hi) in enumerate(CH)]
+        if not me["expect"].get((v, 1)):
+            stages = [(0, range(KT))]
+        for k, tiles in stages:
+            g.tensor.wait_ge(S[FAM[k] + str(v)], me["expect"][(v, k)])
+            for fam, ps, a, b in (("mv", T["ps%d" % (2 * j)], v, h), ("mh", T["ps%d" % (2 * j + 1)], h, v)):
+                for t in tiles:
+                    mm = g.tensor.matmul(ps[0:C, 0:C], xs(a, C * t, C * t + C), xs(b, C * t, C * t + C),
+                                         t == 0, t == KT - 1)
+                if tiles[-1] == KT - 1:
+                    mm.then_inc(S[fam + str(v)], 1)
+        g.vector.wait_ge(S["mv%d" % v], 1)
+        g.vector.tensor_copy(MV[0:C, C * j:C * j + C], T["ps%d" % (2 * j)][0:C, 0:C]).then_inc(S["cv%d" % v], 1)
+        g.vector.wait_ge(S["mh%d" % v], 1)
+        g.vector.tensor_copy(R[0:C, C * v:C * v + C], T["ps%d" % (2 * j + 1)][0:C, 0:C]).then_inc(S["cw%d" % v], 1)
 
-    for v, both, _ in me["vis"]:
-        if both:
-            g.wait_ge(S["cp%d" % v], 1)
-            dsts = [(P[v], R[:, C * h:C * h + C])]
-            if not is_rank:
-                dsts.append((P[h], R[:, C * v:C * v + C]))
-            send(R[:, C * v:C * v + C], dsts, S["rr%d" % ((h + v) % n)], M_ENG, False)
+    if me["vis"]:
+        g.wait_ge(S.ms, fills)
+    for j, v in enumerate(me["vis"]):
+        g.wait_ge(S["cv%d" % v], 1)
+        send(MV[:, C * j:C * j + C], [(P[v], R[:, C * h:C * h + C])], S["rr%d" % ((h + v) % n)], M_ENG, False)
+        if not is_rank:
+            g.wait_ge(S["cw%d" % v], 1)
+            send(R[:, C * v:C * v + C], [(P[h], R[:, C * v:C * v + C])], S["rr%d" % ((h + v) % n)], M_ENG, False)
 
-    stores = 0
     if is_rank:
-        items = [(cls, S["cp%d" % v], 1, 0, v) for v, _, cls in me["vis"]]
-        items += [(cls, S["rr%d" % ((h + p) % n)], M_ENG, half, p) for p, half, cls in me["res"]]
-        items.sort(key=lambda it: (it[0], it[4]))
-        for k, (_, sem, cnt, half, p) in enumerate(items):
-            q = g.sync if k % 2 == 0 else g.scalar
-            q.wait_ge(sem, cnt)
-            q.dma_start(T.y[:, C * p:C * p + C], R[C * half:C * half + C, C * p:C * p + C]).then_inc(S.st, 16)
-            stores += 1
-    if sent[0]:
-        g.wait_ge(S.snd, sent[0])
-    if stores:
-        g.wait_ge(S.st, 16 * stores)
+        g.sync.wait_ge(S.ms, fills)
+        for v in me["vis"]:
+            g.sync.wait_ge(S["cw%d" % v], 1)
+        for p in me["res"]:
+            g.sync.wait_ge(S["rr%d" % ((h + p) % n)], M_ENG)
+        g.sync.dma_start(T.y[:], R[0:C, :]).then_inc(S.st, 16)
+        g.wait_ge(S.st, 16)
+    g.wait_ge(S.snd, sent[0])

from concourse.bass import DstId, RemoteDMATransfer

N, KT, C = 9, 8, 64
W = KT * C

A_ENG = 8
B_ENG = 8
F_ENG = 8
M_ENG = 8
NQ = 3
CUT = 2 * C
CH = ((0, CUT), (CUT, W))
FAM = ("xa", "xb")

SCRATCH = {
    "X": ("sbuf", [128, N * W], "bfloat16"),
    "R": ("sbuf", [128, N * C], "bfloat16"),
    "MV": ("sbuf", [128, 2 * C], "bfloat16"),
}
for _j in range(4):
    SCRATCH["ps%d" % _j] = ("psum", [128, 512], "float32")

SEMAPHORES = ["ld0", "ld1", "ms", "st", "snd"] + [p + str(a) for p in FAM + ("mv", "mh", "cv", "cw", "rr")
                                                  for a in range(N)]
_CACHE = {}


def _cross(pa, pb, mate):
    two = [(x, y) for x in range(len(pb)) for y in range(x + 1, len(pb))]
    best = None
    for code in range(len(two) ** len(pa)):
        rows = []
        for _ in pa:
            rows.append(two[code % len(two)])
            code //= len(two)
        hin = [sum(1 for j in rows[i] if not mate[i][j]) for i in range(len(pa))]
        hin += [sum(1 for i in range(len(pa)) if j not in rows[i] and not mate[i][j]) for j in range(len(pb))]
        out = [sum(1 for j in range(len(pb)) if j not in rows[i] and not mate[i][j]) for i in range(len(pa))]
        out += [sum(1 for i in range(len(pa)) if j in rows[i] and not mate[i][j]) for j in range(len(pb))]
        cost = (max(hin), max(out))
        if best is None or cost < best[0]:
            best = (cost, rows)
    return best[1]


def _plan(T, topo):
    if "role" in _CACHE:
        return _CACHE["role"]
    P = list(T.cores)
    n = len(P)
    ch = [topo.chip(c) for c in P]
    every = range(topo.CORES_PER_CHIP * topo.CHIPS)
    planes = []
    for r in range(n):
        for pl in planes:
            if topo.same_plane(ch[pl[0]], ch[r]):
                pl.append(r)
                break
        else:
            planes.append([r])
    role = {}

    def node(c, h):
        if c not in role:
            role[c] = {"home": h, "calls": [], "expect": {}, "vis": [], "res": []}
        return role[c]

    def arrive(c, a, k, cnt):
        role[c]["expect"][(a, k)] = role[c]["expect"].get((a, k), 0) + cnt

    def host(c, h, v):
        node(c, h)["vis"].append(v)
        role[P[v]]["res"].append(h)
        if c != P[h]:
            role[P[h]]["res"].append(v)

    for r in range(n):
        node(P[r], r)

    def ports(r):
        far = [P[s] for s in range(n) if s != r and not topo.same_plane(ch[r], ch[s])]
        own = [c for c in every if topo.chip(c) == ch[r] and c != P[r] and all(topo.may_write(c, o) for o in far)]
        return sorted(own, key=lambda c: (topo.die(c) == topo.die(P[r]), c))

    hosted = {r: [] for r in range(n)}
    visits = {r: [] for r in range(n)}
    pa, pb = planes
    rows = _cross(pa, pb, [[topo.mates(ch[a], ch[b]) for b in pb] for a in pa])
    for i, a in enumerate(pa):
        for j, b in enumerate(pb):
            h, v = (a, b) if j in rows[i] else (b, a)
            hosted[h].append(v)
            visits[v].append(h)
    Q = {}
    for r in range(n):
        Q[r] = ports(r)[:min(NQ, max(len(hosted[r]), len(visits[r])))]
        for c in Q[r]:
            node(c, r)
        for k, (lo, hi) in enumerate(CH):
            role[P[r]]["calls"].append((k, lo, hi, list(Q[r]), A_ENG, True))
            for c in Q[r]:
                arrive(c, r, k, A_ENG)
    for v in range(n):
        q = len(Q[v])
        tgt = [Q[h][hosted[h].index(v) % len(Q[h])] for h in sorted(visits[v], key=lambda s: topo.mates(ch[v], ch[s]))]
        jobs = [(tgt[i::q], [c]) for i, c in enumerate(Q[v])]
        if len(tgt) < q:
            jobs = jobs[:len(tgt) - 1] + [([tgt[-1]], Q[v][len(tgt) - 1:])]
        for to, cs in jobs:
            for k, (lo, hi) in enumerate(CH):
                cs_k = cs if k == 0 else cs[:1]
                step = (hi - lo) // len(cs_k)
                for i, c in enumerate(cs_k):
                    role[c]["calls"].append((k, lo + i * step, lo + (i + 1) * step, to, F_ENG, False))
                    for t in to:
                        arrive(t, v, k, F_ENG)
    for pl in planes:
        m = len(pl)
        for i in range(m):
            to = [pl[(i + d) % m] for d in range(1, m) if 2 * d < m or (2 * d == m and i < d)]
            role[P[pl[i]]]["calls"].append((0, 0, W, [P[s] for s in to], B_ENG, False))
            for s in to:
                arrive(P[s], pl[i], 0, B_ENG)
                host(P[s], s, pl[i])
    for h in range(n):
        for i, v in enumerate(hosted[h]):
            host(Q[h][i % len(Q[h])], h, v)
    _CACHE["role"] = role
    return role


def rank_program(g, core, T, topo):
    role = _plan(T, topo)
    me = role.get(core)
    if me is None:
        return
    P = list(T.cores)
    n = len(P)
    h = me["home"]
    is_rank = core == P[h]
    X, R, MV, S = T.X, T.R, T.MV, T.sem
    sent = [0]
    lq = (g.sync, g.scalar)
    leaves = topo.mask(core, P[(h + 1) % n])

    def xs(a, lo=0, hi=W):
        return X[:, a * W + lo:a * W + hi]

    def send(src, dsts, sem, neng, high):
        m = -1
        for d, _ in dsts:
            m &= topo.mask(core, d)
        eng = [b for b in range(m.bit_length()) if (m >> b) & 1]
        stay = [b for b in eng if not (leaves >> b) & 1]
        if high and neng <= len(stay):
            eng = stay
        eng = eng[:neng]
        ids = [DstId(rid=topo.addr(d)[0], pnc=topo.addr(d)[1]) for d, _ in dsts]
        tr = RemoteDMATransfer(dst_ids=ids, dma_engine_mask=sum(1 << b for b in eng), remote_sem=sem,
                               srcs=[src], dsts=[ap for _, ap in dsts], alu_op=0)
        g.remote_dma_fused([tr], local_sem=S.snd)
        sent[0] += neng

    fills = 0
    if me["vis"]:
        g.vector.memset(MV[C:2 * C, :], 0.0).then_inc(S.ms, 1)
        fills += 1
    if is_rank:
        g.vector.memset(R[0:C, C * h:C * h + C], 0.0).then_inc(S.ms, 1)
        fills += 1
    else:
        for v in me["vis"]:
            g.vector.memset(R[C:2 * C, C * v:C * v + C], 0.0).then_inc(S.ms, 1)
            fills += 1

    if is_rank:
        home = [(S["ld%d" % k], 16) for k in range(len(CH))]
        for k, (lo, hi) in enumerate(CH):
            lq[k].dma_start(xs(h, lo, hi), T.x[:, lo:hi]).then_inc(*home[k])
    else:
        home = [(S[FAM[k] + str(h)], me["expect"][(h, k)]) for k in range(len(CH))]
    got = set()
    for k, lo, hi, dsts, neng, high in me["calls"]:
        for c, (a, b) in enumerate(CH):
            if lo < b and hi > a and c not in got:
                g.wait_ge(*home[c])
                got.add(c)
        send(xs(h, lo, hi), [(d, xs(h, lo, hi)) for d in dsts], S[FAM[k] + str(h)], neng, high)

    if me["vis"]:
        for w in home:
            g.tensor.wait_ge(*w)
    for j, v in enumerate(me["vis"]):
        stages = [(k, range(lo // C, hi // C)) for k, (lo, hi) in enumerate(CH)]
        if not me["expect"].get((v, 1)):
            stages = [(0, range(KT))]
        for k, tiles in stages:
            g.tensor.wait_ge(S[FAM[k] + str(v)], me["expect"][(v, k)])
            for fam, ps, a, b in (("mv", T["ps%d" % (2 * j)], v, h), ("mh", T["ps%d" % (2 * j + 1)], h, v)):
                for t in tiles:
                    mm = g.tensor.matmul(ps[0:C, 0:C], xs(a, C * t, C * t + C), xs(b, C * t, C * t + C),
                                         t == 0, t == KT - 1)
                if tiles[-1] == KT - 1:
                    mm.then_inc(S[fam + str(v)], 1)
        g.vector.wait_ge(S["mv%d" % v], 1)
        g.vector.tensor_copy(MV[0:C, C * j:C * j + C], T["ps%d" % (2 * j)][0:C, 0:C]).then_inc(S["cv%d" % v], 1)
        g.vector.wait_ge(S["mh%d" % v], 1)
        g.vector.tensor_copy(R[0:C, C * v:C * v + C], T["ps%d" % (2 * j + 1)][0:C, 0:C]).then_inc(S["cw%d" % v], 1)

    if me["vis"]:
        g.wait_ge(S.ms, fills)
    for j, v in enumerate(me["vis"]):
        g.wait_ge(S["cv%d" % v], 1)
        send(MV[:, C * j:C * j + C], [(P[v], R[:, C * h:C * h + C])], S["rr%d" % ((h + v) % n)], M_ENG, False)
        if not is_rank:
            g.wait_ge(S["cw%d" % v], 1)
            send(R[:, C * v:C * v + C], [(P[h], R[:, C * v:C * v + C])], S["rr%d" % ((h + v) % n)], M_ENG, False)

    if is_rank:
        g.sync.wait_ge(S.ms, fills)
        for v in me["vis"]:
            g.sync.wait_ge(S["cw%d" % v], 1)
        for p in me["res"]:
            g.sync.wait_ge(S["rr%d" % ((h + p) % n)], M_ENG)
        g.sync.dma_start(T.y[:], R[0:C, :]).then_inc(S.st, 16)
        g.wait_ge(S.st, 16)
    g.wait_ge(S.snd, sent[0])
